import numpy as np
CORES = [56,64,184,192,312,320,440,448]
N = 8
R, T = 4096, 1024
HOST = [c // 128 for c in CORES]
G = [[r for r in range(N) if HOST[r] == h] for h in sorted(set(HOST))]
H = len(G); K = [sorted(set(HOST)).index(h) for h in HOST]
def entries(a): return a.T.reshape(-1)
def pack(v, P): return np.ascontiguousarray(np.asarray(v, np.int32).reshape(-1, P).T)
def among(rng, a): return rng.permutation(np.concatenate([a, rng.choice(a, T - len(a))]))
def lists(rng, how):
    O = np.stack([among(rng, np.arange(N)) for g in G])
    if how == "away": O = np.stack([among(rng, [r for r in range(N) if r not in g]) for g in G])
    if how == "home": O = np.stack([among(rng, g) for g in G])
    J = rng.integers(0, R, (H, T)); J[:, rng.integers(T)] = rng.permutation(R)[:H]
    if how == "distinct": O[:], J = rng.integers(N), rng.permutation(R)[:H * T].reshape(H, T)
    if how == "hotrank":
        s = rng.integers(1, H); O[:] = np.array([rng.choice(G[(k + s) % H]) for k in range(H)])[:, None]; J = np.stack([rng.permutation(R)[:T] for g in G])
    I = R * O + J
    if how == "edge":
        C, Q = rng.integers(0, 2 * N, (H, T)), rng.permutation(T)
        C[:, Q[:2 * N]] = np.stack([rng.permutation(2 * N) for g in G]); C[:, Q[2 * N]] = rng.permutation(2 * N)[:H]
        I = R * (C // 2) + (R - 1) * (C % 2)
    return {"idx": np.stack([pack(I[K[r]], 16) for r in range(N)])}
def setup_inputs(rng):
    return dict({"tab": rng.standard_normal((N, 128, R), dtype=np.float32)}, **lists(rng, "uniform"))
def setup_inputs_away(rng):
    d = setup_inputs(rng); d.update(lists(rng, "away"))
    for k in ("tab",): d[k] = (d[k].astype(np.float32) * 1048576.0).astype(d[k].dtype)
    return d
def setup_inputs_distinct(rng):
    d = setup_inputs(rng); d.update(lists(rng, "distinct"))
    for k in ("tab",): d[k] = (d[k].astype(np.float32) * (1 / 1024.0)).astype(d[k].dtype)
    return d
def setup_inputs_edge(rng):
    d = setup_inputs(rng); d.update(lists(rng, "edge"))
    return d
def setup_inputs_home(rng):
    d = setup_inputs(rng); d.update(lists(rng, "home"))
    return d
def setup_inputs_hotrank(rng):
    d = setup_inputs(rng); d.update(lists(rng, "hotrank"))
    return d
def check_inputs(x):
    bad = []
    if x["idx"].min() < 0 or x["idx"].max() >= N * R: bad.append("idx out of range")
    if any((x["idx"][r] != x["idx"][s]).any() for r in range(N) for s in range(r) if HOST[r] == HOST[s]): bad.append("two ranks of one host hold different lists")
    return bad
def reference(tab, idx):
    A = np.concatenate(list(tab), axis=1)
    return {"y": np.stack([A[:, entries(idx[r])] for r in range(N)])}

@@ -1,0 +1,227 @@
+from concourse.bass import DstId, RemoteDMATransfer
+from concourse.mybir import dt, AluOpType, ActivationFunctionType
+
+ROWS, COLS, ENT = 128, 4096, 1024
+Q, HALF = 256, 512
+LC = 64
+
+SCRATCH = {
+    "tabw": ("sbuf", [128, COLS + 8], "float32"),
+    "lo": ("sbuf", [128, LC], "int32"), "lr": ("sbuf", [128, LC], "int32"),
+    "lc": ("sbuf", [128, LC], "int32"), "ld": ("sbuf", [128, LC], "int32"),
+    "to": ("sbuf", [128, LC], "int32"), "tr": ("sbuf", [128, LC], "int32"),
+    "tc": ("sbuf", [128, LC], "int32"), "td": ("sbuf", [128, LC], "int32"),
+    "oo": ("sbuf", [128, LC], "uint16"), "orr": ("sbuf", [128, LC], "uint16"),
+    "oc": ("sbuf", [128, LC], "uint16"), "od": ("sbuf", [128, LC], "uint16"),
+    "go": ("sbuf", [128, ENT], "float32"), "gr": ("sbuf", [128, ENT], "float32"),
+    "gc4": ("sbuf", [128, ENT], "float32"), "gd": ("sbuf", [128, ENT], "float32"),
+    "jp": ("sbuf", [128, LC], "int32"), "jc": ("sbuf", [128, LC], "int32"), "jq": ("sbuf", [128, LC], "int32"),
+    "jj": ("sbuf", [128, LC], "int32"), "sd": ("sbuf", [128, LC], "int32"), "sm": ("sbuf", [128, LC], "int32"),
+    "ss": ("sbuf", [128, LC], "int32"), "sel": ("sbuf", [128, LC], "uint16"),
+    "fa": ("sbuf", [128, 2 * HALF], "float32"), "fb": ("sbuf", [128, 2 * HALF], "float32"),
+    "yb": ("sbuf", [128, ENT], "float32"),
+    "yr": ("sbuf", [128, Q], "float32"), "yc": ("sbuf", [128, Q], "float32"), "yd": ("sbuf", [128, Q], "float32"),
+    "xo": ("sbuf", [128, HALF], "float32"), "xs": ("sbuf", [128, HALF], "float32"),
+    "xc": ("sbuf", [128, HALF], "float32"), "xp": ("sbuf", [128, HALF], "float32"),
+}
+SEMAPHORES = ["sidx", "stab", "sio", "vf", "vq", "slr", "slc", "sld", "ls",
+              "foo", "for_", "foc", "fod", "ho", "hr", "hc", "hd", "ssel",
+              "syr", "syc", "syd", "sxo", "sxs", "sxc", "sxp", "sfa", "sfb", "sya", "syb", "sst"]
+
+
+def place(topo, c):
+    return (topo.host(c), topo.chip(c))
+
+
+def neighbours(T, topo, r):
+    me, out = T.cores[r], {}
+    for c in T.cores:
+        if c == me:
+            continue
+        if topo.host(c) == topo.host(me):
+            out["twin"] = c
+        elif topo.chip(c) == topo.chip(me):
+            if topo.rack(topo.host(c)) == topo.rack(topo.host(me)):
+                out["rack"] = c
+            elif topo.may_write(me, c):
+                out["cable"] = c
+    return out
+
+
+def helpers(T, topo, rc, twin):
+    per = 512 // 4
+    base = topo.host(rc) * per
+    chip = [c for c in range(base, base + per) if topo.chip(c) == topo.chip(rc) and c != rc]
+    quarter, merge = [], []
+    for d in (topo.die(rc), 1 - topo.die(rc)):
+        mine = [c for c in chip if topo.die(c) == d]
+        x = [c for c in mine if topo.may_write(c, twin)][0]
+        quarter += [[c for c in mine if not topo.may_write(c, twin)][0], x]
+        merge.append(x)
+    return quarter, merge
+
+
+def split(mask, n):
+    bits = [b for b in range(16) if mask >> b & 1]
+    k = len(bits) // n
+    return [sum(1 << b for b in bits[i * k:(i + 1) * k]) for i in range(n)]
+
+
+def count(mask):
+    return sum(mask >> b & 1 for b in range(16))
+
+
+def send(g, topo, core, local, parts):
+    trs, n = [], 0
+    for dst, srcs, out, sem, mask in parts:
+        rid, pid = topo.addr(dst, core)
+        trs.append(RemoteDMATransfer(dst_ids=[DstId(rid=rid, pnc=pid)], dma_engine_mask=mask, remote_sem=sem,
+                                     srcs=srcs, dsts=[out], alu_op=1 if len(srcs) > 1 else 0))
+        n += count(mask)
+    g.remote_dma_fused(trs, local_sem=local)
+    return n
+
+
+def rank_core(g, core, T, topo, rank):
+    S, nb = T.sem, neighbours(T, topo, rank)
+    rack, cable, twin = nb["rack"], nb["cable"], nb["twin"]
+    quarter, merge = helpers(T, topo, core, twin)
+    rquarter = helpers(T, topo, rack, neighbours(T, topo, T.cores.index(rack))["twin"])[0]
+    v, s = g.vector, g.scalar
+    add, mult, mx, mn = AluOpType.add, AluOpType.mult, AluOpType.max, AluOpType.min
+
+    for k in range(8):
+        (g.sync if k % 2 == 0 else s).dma_start(T.lo[16 * k:16 * k + 16, :], T.idx[:]).then_inc(S.sidx, 16)
+    g.sync.dma_start(T.tabw[0:64, 4:4 + COLS], T.tab[0:64, :]).then_inc(S.stab, 16)
+    s.dma_start(T.tabw[64:128, 4:4 + COLS], T.tab[64:128, :]).then_inc(S.stab, 16)
+
+    g.iota(T.jp[:], [[0, LC]], 0, 1).then_inc(S.sio, 1)
+    g.iota(T.jc[:], [[0, 2], [16, LC // 2]], 0, 0).then_inc(S.sio, 1)
+    off = topo.mask(core, rack) & topo.mask(core, cable)
+    onc = topo.mask(core, merge[0])
+    rest = onc & ~off
+    n = 0
+    g.wait_ge(S.sidx, 128)
+    m = split(off, 2)
+    n += send(g, topo, core, S.ls, [(rack, [T.lo[:]], T.lr[:], S.slr, m[0]), (cable, [T.lo[:]], T.lc[:], S.slc, m[1])])
+    g.wait_ge(S.slc, count(m[1]))
+    n += send(g, topo, core, S.ls, [(rack, [T.lc[:]], T.ld[:], S.sld, off)])
+
+    nq = [0]
+
+    def chain(ins):
+        ins.then_inc(S.vq, 1)
+        nq[0] += 1
+        v.wait_ge(S.vq, nq[0])
+
+    v.memset(T.tabw[:, 0:4], -0.0).then_inc(S.vf, 1)
+    v.memset(T.tabw[:, 4 + COLS:8 + COLS], -0.0).then_inc(S.vf, 1)
+
+    def offsets(lst, tmp, out, sem):
+        chain(v.tensor_scalar(tmp[:], lst[:], float(1 - COLS * rank), 0.0, add, mx))
+        v.tensor_scalar(out[:], tmp[:], float(COLS + 1), None, mn).then_inc(sem, 1)
+
+    v.wait_ge(S.sidx, 128)
+    offsets(T.lo, T.to, T.oo, S.foo)
+    v.wait_ge(S.sio, 2)
+    chain(v.tensor_scalar(T.jq[:], T.jp[:], 15, None, AluOpType.bitwise_and))
+    chain(v.tensor_tensor(T.jj[:], T.jq[:], T.jc[:], add))
+    chain(v.tensor_scalar(T.sd[:], T.lo[:], 12, 1, AluOpType.logical_shift_right, AluOpType.bitwise_and))
+    mine = rank % 2
+    chain(v.tensor_scalar(T.sm[:], T.sd[:], float(HALF if mine == 0 else -HALF), float(0 if mine == 0 else HALF), mult, add))
+    chain(v.tensor_tensor(T.ss[:], T.jj[:], T.sm[:], add))
+    v.tensor_copy(T.sel[:], T.ss[:]).then_inc(S.ssel, 1)
+    v.wait_ge(S.slr, count(m[0]))
+    offsets(T.lr, T.tr, T.orr, S.for_)
+    v.wait_ge(S.slc, count(m[1]))
+    offsets(T.lc, T.tc, T.oc, S.foc)
+    v.wait_ge(S.vf, 2)
+    v.wait_ge(S.stab, 32)
+    s.wait_ge(S.vf, 2)
+    s.wait_ge(S.stab, 32)
+    win = T.tabw[:, 3:5 + COLS]
+    h = LC // 2
+
+    def gather(o, out, ready, done):
+        v.wait_ge(ready, 1)
+        v.tensor_copy(out[:, 0:HALF], win.indirect(o[:, 0:h])).then_inc(done, 1)
+        s.wait_ge(ready, 1)
+        s.activation(out[:, HALF:ENT], win.indirect(o[:, h:LC]), ActivationFunctionType.Copy).then_inc(done, 1)
+        g.wait_ge(done, 2)
+
+    def qs(t, k):
+        return [t[:, Q * k:Q * k + Q]]
+
+    gather(T.orr, T.gr, S.for_, S.hr)
+    m = split(onc, 4)
+    n += send(g, topo, core, S.ls, [(quarter[k], qs(T.gr, k), T.yr[:], S.syr, m[k]) for k in range(4)])
+    gather(T.oc, T.gc4, S.foc, S.hc)
+    m = split(rest, 4)
+    n += send(g, topo, core, S.ls, [(quarter[k], qs(T.gc4, k), T.yc[:], S.syc, m[k]) for k in range(4)])
+    v.wait_ge(S.sld, count(off))
+    offsets(T.ld, T.td, T.od, S.fod)
+    gather(T.od, T.gd, S.fod, S.hd)
+    m = split(off, 4)
+    n += send(g, topo, core, S.ls, [(rquarter[k], qs(T.gd, k), T.yd[:], S.syd, m[k]) for k in range(4)])
+    gather(T.oo, T.go, S.foo, S.ho)
+    m = split(rest, 2)
+    n += send(g, topo, core, S.ls, [(merge[k], [T.go[:, HALF * k:HALF * k + HALF]], T.xo[:], S.sxo, m[k]) for k in range(2)])
+    g.wait_ge(S.ls, n)
+
+    got = count(off) + count(rest)
+    v.wait_ge(S.ssel, 1)
+    v.wait_ge(S.sfa, got)
+    v.tensor_copy(T.yb[:, 0:HALF], T.fa[:].indirect(T.sel[:, 0:h])).then_inc(S.sya, 1)
+    s.wait_ge(S.ssel, 1)
+    s.wait_ge(S.sfb, got)
+    s.activation(T.yb[:, HALF:ENT], T.fb[:].indirect(T.sel[:, h:LC]), ActivationFunctionType.Copy).then_inc(S.syb, 1)
+    s.wait_ge(S.syb, 1)
+    s.dma_start(T.y[:, HALF:ENT], T.yb[:, HALF:ENT]).then_inc(S.sst, 16)
+    g.sync.wait_ge(S.sya, 1)
+    g.sync.dma_start(T.y[:, 0:HALF], T.yb[:, 0:HALF]).then_inc(S.sst, 16)
+    g.sync.wait_ge(S.sst, 32)
+
+
+def helper_core(g, core, T, topo, rank):
+    S, nb = T.sem, neighbours(T, topo, rank)
+    rc, rack, cable, twin = T.cores[rank], nb["rack"], nb["cable"], nb["twin"]
+    quarter, merge = helpers(T, topo, rc, twin)
+    if core not in quarter:
+        return
+    k = quarter.index(core)
+    xr = helpers(T, topo, rack, neighbours(T, topo, T.cores.index(rack))["twin"])[1][k // 2]
+    xc = helpers(T, topo, cable, neighbours(T, topo, T.cores.index(cable))["twin"])[1][k // 2]
+    lo = Q * (k % 2)
+    n = 0
+    off0 = topo.mask(rc, rack) & topo.mask(rc, cable)
+    onc0 = topo.mask(rc, merge[0])
+    rest0 = onc0 & ~off0
+    g.wait_ge(S.syr, count(onc0) // 4)
+    moff = topo.mask(core, xr)
+    n += send(g, topo, core, S.ls, [(xr, [T.yr[:]], T.xs[:, lo:lo + Q], S.sxs, moff)])
+    g.wait_ge(S.syc, count(rest0) // 4)
+    g.wait_ge(S.syd, count(off0) // 4)
+    n += send(g, topo, core, S.ls, [(xc, [T.yc[:], T.yd[:]], T.xc[:, lo:lo + Q], S.sxc, topo.mask(core, xc))])
+    if core in merge:
+        half = merge.index(core)
+        land, sem = ((T.fa, S.sfa), (T.fb, S.sfb))[half]
+        v = g.vector
+        v.wait_ge(S.sxo, count(rest0) // 2)
+        v.wait_ge(S.sxs, 2 * count(moff))
+        v.tensor_tensor(T.xp[:], T.xo[:], T.xs[:], AluOpType.add).then_inc(S.sxp, 1)
+        g.wait_ge(S.sxp, 1)
+        g.wait_ge(S.sxc, 2 * count(topo.mask(core, xc)))
+        mt = topo.mask(core, twin)
+        n += send(g, topo, core, S.ls, [(twin, [T.xp[:], T.xc[:]], land[:, HALF:2 * HALF], sem, mt)])
+        n += send(g, topo, core, S.ls, [(rc, [T.xp[:], T.xc[:]], land[:, 0:HALF], sem, topo.mask(core, rc) & ~mt)])
+    g.wait_ge(S.ls, n)
+
+
+def rank_program(g, core, T, topo):
+    rank = T.rank_of(core)
+    if rank is not None:
+        rank_core(g, core, T, topo, rank)
+        return
+    for r in range(len(T.cores)):
+        if place(topo, T.cores[r]) == place(topo, core):
+            helper_core(g, core, T, topo, r)

@@ -4,6 +4,8 @@ from concourse.mybir import dt, AluOpType, ActivationFunctionType
 ROWS, COLS, ENT = 128, 4096, 1024
 Q, HALF = 256, 512
 LC = 64
+SCHED = [("c", (0, 1), "rest", ()), ("c", (2, 3), "rest", ()), ("d", (0, 1), "off", ()), ("d", (2, 3), "off", ()),
+         ("r", (2,), "rest", ()), ("x", (0, 1), "off", (2,)), ("o", (0, 1), "rest", (1,)), ("o", (2, 3), "all", (4,))]
 
 SCRATCH = {
     "tabw": ("sbuf", [128, COLS + 8], "float32"),
@@ -18,15 +20,21 @@ SCRATCH = {
     "jp": ("sbuf", [128, LC], "int32"), "jc": ("sbuf", [128, LC], "int32"), "jq": ("sbuf", [128, LC], "int32"),
     "jj": ("sbuf", [128, LC], "int32"), "sd": ("sbuf", [128, LC], "int32"), "sm": ("sbuf", [128, LC], "int32"),
     "ss": ("sbuf", [128, LC], "int32"), "sel": ("sbuf", [128, LC], "uint16"),
-    "fa": ("sbuf", [128, 2 * HALF], "float32"), "fb": ("sbuf", [128, 2 * HALF], "float32"),
+    "f0": ("sbuf", [128, 2 * Q], "float32"), "f1": ("sbuf", [128, 2 * Q], "float32"),
+    "f2": ("sbuf", [128, 2 * Q], "float32"), "f3": ("sbuf", [128, 2 * Q], "float32"),
     "yb": ("sbuf", [128, ENT], "float32"),
-    "yr": ("sbuf", [128, Q], "float32"), "yc": ("sbuf", [128, Q], "float32"), "yd": ("sbuf", [128, Q], "float32"),
-    "xo": ("sbuf", [128, HALF], "float32"), "xs": ("sbuf", [128, HALF], "float32"),
-    "xc": ("sbuf", [128, HALF], "float32"), "xp": ("sbuf", [128, HALF], "float32"),
+    "dl": ("dram", [8, 128, 1], "int32"), "dr": ("dram", [8, 128, 1], "int32"),
+    "dq": ("dram", [2, 128, 1], "int32"),
+    "yc": ("sbuf", [128, Q], "float32"), "yd": ("sbuf", [128, Q], "float32"),
+    "yr": ("sbuf", [128, HALF], "float32"),
+    "xo": ("sbuf", [128, Q], "float32"), "xs": ("sbuf", [128, Q], "float32"),
+    "xc": ("sbuf", [128, Q], "float32"), "xp": ("sbuf", [128, Q], "float32"),
 }
-SEMAPHORES = ["sidx", "stab", "sio", "vf", "vq", "slr", "slc", "sld", "ls",
+SEMAPHORES = ["sidx", "stab", "sio", "vf", "vq", "slr", "slc", "sld", "ls", "sdl", "sdr", "sdq",
+              "k0", "k1", "k2", "k3", "k4", "k5", "k6", "k7", "k8", "k9",
               "foo", "for_", "foc", "fod", "ho", "hr", "hc", "hd", "ssel",
-              "syr", "syc", "syd", "sxo", "sxs", "sxc", "sxp", "sfa", "sfb", "sya", "syb", "sst"]
+              "syr", "syc", "syd", "sxo", "sxs", "sxc", "sxp", "sf0", "sf1", "sf2", "sf3",
+              "sy0", "sy1", "sy2", "sy3", "sst"]
 
 
 def place(topo, c):
@@ -48,17 +56,24 @@ def neighbours(T, topo, r):
     return out
 
 
-def helpers(T, topo, rc, twin):
+def roles(T, topo, rc):
+    twin = neighbours(T, topo, T.cores.index(rc))["twin"]
     per = 512 // 4
     base = topo.host(rc) * per
     chip = [c for c in range(base, base + per) if topo.chip(c) == topo.chip(rc) and c != rc]
-    quarter, merge = [], []
+    quarter, merge, other = [], [], []
     for d in (topo.die(rc), 1 - topo.die(rc)):
-        mine = [c for c in chip if topo.die(c) == d]
-        x = [c for c in mine if topo.may_write(c, twin)][0]
-        quarter += [[c for c in mine if not topo.may_write(c, twin)][0], x]
-        merge.append(x)
-    return quarter, merge
+        own = [c for c in chip if topo.die(c) == d and topo.may_write(c, twin)]
+        non = [c for c in chip if topo.die(c) == d and not topo.may_write(c, twin)]
+        quarter += [non[0], own[0]]
+        merge += own
+        other += non[1:]
+    return quarter, merge, other[0]
+
+
+def everyone(T, topo, rc):
+    q, m, p = roles(T, topo, rc)
+    return q + [c for c in m if c not in q] + [p]
 
 
 def split(mask, n):
@@ -69,6 +84,16 @@ def split(mask, n):
 
 def count(mask):
     return sum(mask >> b & 1 for b in range(16))
+
+
+def masks(topo, rc, rack, cable, helper):
+    off = topo.mask(rc, rack) & topo.mask(rc, cable)
+    onc = topo.mask(rc, helper)
+    return {"all": onc, "off": off, "rest": onc & ~off}
+
+
+def engines(MM, block, k):
+    return [count(MM[mk]) // len(qq) for b, qq, mk, hold in SCHED if b == block and k in qq][0]
 
 
 def send(g, topo, core, local, parts):
@@ -85,26 +110,33 @@ def send(g, topo, core, local, parts):
 def rank_core(g, core, T, topo, rank):
     S, nb = T.sem, neighbours(T, topo, rank)
     rack, cable, twin = nb["rack"], nb["cable"], nb["twin"]
-    quarter, merge = helpers(T, topo, core, twin)
-    rquarter = helpers(T, topo, rack, neighbours(T, topo, T.cores.index(rack))["twin"])[0]
+    quarter, merge, passer = roles(T, topo, core)
+    rquarter, rmerge, _ = roles(T, topo, rack)
     v, s = g.vector, g.scalar
     add, mult, mx, mn = AluOpType.add, AluOpType.mult, AluOpType.max, AluOpType.min
 
     for k in range(8):
         (g.sync if k % 2 == 0 else s).dma_start(T.lo[16 * k:16 * k + 16, :], T.idx[:]).then_inc(S.sidx, 16)
+    g.sync.dma_start(T.dl[:], T.idx[:]).then_inc(S.sdl, 16)
     g.sync.dma_start(T.tabw[0:64, 4:4 + COLS], T.tab[0:64, :]).then_inc(S.stab, 16)
     s.dma_start(T.tabw[64:128, 4:4 + COLS], T.tab[64:128, :]).then_inc(S.stab, 16)
+    hs = everyone(T, topo, core)
+    g.sync.wait_ge(S.sdr, len(hs) * count(topo.mask(rack, core)))
+    for k in range(8):
+        g.sync.dma_start(T.lr[16 * k:16 * k + 16, :], T.dr[:]).then_inc(S.slr, 16)
 
     g.iota(T.jp[:], [[0, LC]], 0, 1).then_inc(S.sio, 1)
-    g.iota(T.jc[:], [[0, 2], [16, LC // 2]], 0, 0).then_inc(S.sio, 1)
-    off = topo.mask(core, rack) & topo.mask(core, cable)
-    onc = topo.mask(core, merge[0])
-    rest = onc & ~off
+    g.iota(T.jc[:], [[0, 2], [0, 2], [16, LC // 4]], 0, 0).then_inc(S.sio, 1)
+    MM = masks(topo, core, rack, cable, merge[0])
+    off = MM["off"]
     n = 0
     g.wait_ge(S.sidx, 128)
-    m = split(off, 2)
-    n += send(g, topo, core, S.ls, [(rack, [T.lo[:]], T.lr[:], S.slr, m[0]), (cable, [T.lo[:]], T.lc[:], S.slc, m[1])])
-    g.wait_ge(S.slc, count(m[1]))
+    n += send(g, topo, core, S.ls, [(cable, [T.lo[:]], T.lc[:], S.slc, off)])
+    g.wait_ge(S.sdl, 16)
+    m = split(MM["rest"], 8)
+    last = len(hs) - 1
+    n += send(g, topo, core, S.ls, [(hs[min(k, last)], [T.dl[k]], T.dq[k - min(k, last)], S.sdq, m[k]) for k in range(8)])
+    g.wait_ge(S.slc, count(off))
     n += send(g, topo, core, S.ls, [(rack, [T.lc[:]], T.ld[:], S.sld, off)])
 
     nq = [0]
@@ -128,92 +160,108 @@ def rank_core(g, core, T, topo, rank):
     chain(v.tensor_tensor(T.jj[:], T.jq[:], T.jc[:], add))
     chain(v.tensor_scalar(T.sd[:], T.lo[:], 12, 1, AluOpType.logical_shift_right, AluOpType.bitwise_and))
     mine = rank % 2
-    chain(v.tensor_scalar(T.sm[:], T.sd[:], float(HALF if mine == 0 else -HALF), float(0 if mine == 0 else HALF), mult, add))
+    chain(v.tensor_scalar(T.sm[:], T.sd[:], float(Q if mine == 0 else -Q), float(0 if mine == 0 else Q), mult, add))
     chain(v.tensor_tensor(T.ss[:], T.jj[:], T.sm[:], add))
     v.tensor_copy(T.sel[:], T.ss[:]).then_inc(S.ssel, 1)
-    v.wait_ge(S.slr, count(m[0]))
-    offsets(T.lr, T.tr, T.orr, S.for_)
-    v.wait_ge(S.slc, count(m[1]))
-    offsets(T.lc, T.tc, T.oc, S.foc)
-    v.wait_ge(S.vf, 2)
-    v.wait_ge(S.stab, 32)
-    s.wait_ge(S.vf, 2)
-    s.wait_ge(S.stab, 32)
     win = T.tabw[:, 3:5 + COLS]
     h = LC // 2
+    done = {"c": S.hc, "d": S.hd, "r": S.hr, "x": S.hr, "o": S.ho}
 
-    def gather(o, out, ready, done):
+    def gather(b, o, out, ready):
         v.wait_ge(ready, 1)
-        v.tensor_copy(out[:, 0:HALF], win.indirect(o[:, 0:h])).then_inc(done, 1)
+        v.tensor_copy(out[:, 0:HALF], win.indirect(o[:, 0:h])).then_inc(done[b], 1)
         s.wait_ge(ready, 1)
-        s.activation(out[:, HALF:ENT], win.indirect(o[:, h:LC]), ActivationFunctionType.Copy).then_inc(done, 1)
-        g.wait_ge(done, 2)
+        s.activation(out[:, HALF:ENT], win.indirect(o[:, h:LC]), ActivationFunctionType.Copy).then_inc(done[b], 1)
 
-    def qs(t, k):
-        return [t[:, Q * k:Q * k + Q]]
-
-    gather(T.orr, T.gr, S.for_, S.hr)
-    m = split(onc, 4)
-    n += send(g, topo, core, S.ls, [(quarter[k], qs(T.gr, k), T.yr[:], S.syr, m[k]) for k in range(4)])
-    gather(T.oc, T.gc4, S.foc, S.hc)
-    m = split(rest, 4)
-    n += send(g, topo, core, S.ls, [(quarter[k], qs(T.gc4, k), T.yc[:], S.syc, m[k]) for k in range(4)])
+    v.wait_ge(S.slc, count(off))
+    offsets(T.lc, T.tc, T.oc, S.foc)
+    for e in (v, s):
+        e.wait_ge(S.vf, 2)
+        e.wait_ge(S.stab, 32)
+    gather("c", T.oc, T.gc4, S.foc)
     v.wait_ge(S.sld, count(off))
     offsets(T.ld, T.td, T.od, S.fod)
-    gather(T.od, T.gd, S.fod, S.hd)
-    m = split(off, 4)
-    n += send(g, topo, core, S.ls, [(rquarter[k], qs(T.gd, k), T.yd[:], S.syd, m[k]) for k in range(4)])
-    gather(T.oo, T.go, S.foo, S.ho)
-    m = split(rest, 2)
-    n += send(g, topo, core, S.ls, [(merge[k], [T.go[:, HALF * k:HALF * k + HALF]], T.xo[:], S.sxo, m[k]) for k in range(2)])
+    gather("d", T.od, T.gd, S.fod)
+    v.wait_ge(S.slr, 128)
+    offsets(T.lr, T.tr, T.orr, S.for_)
+    gather("r", T.orr, T.gr, S.for_)
+    gather("o", T.oo, T.go, S.foo)
+
+    to = {"c": (quarter, T.gc4, T.yc, S.syc), "d": (rquarter, T.gd, T.yd, S.syd), "x": (rmerge, T.gr, T.xs, S.sxs),
+          "o": (merge, T.go, T.xo, S.sxo)}
+    left = []
+    for i, (b, qq, mk, hold) in enumerate(SCHED):
+        g.wait_ge(done[b], 2)
+        for x in hold:
+            g.wait_ge(S["k%d" % x], left[x])
+            left[x] = 0
+        m = split(MM[mk], len(qq))
+        if b == "r":
+            parts = [(passer, [T.gr[:, Q * qq[0]:Q * qq[0] + HALF]], T.yr[:], S.syr, m[0])]
+        else:
+            cs, src, land, sem = to[b]
+            parts = [(cs[k], [src[:, Q * k:Q * k + Q]], land[:], sem, m[a]) for a, k in enumerate(qq)]
+        left.append(send(g, topo, core, S["k%d" % i], parts))
+    for x, c in enumerate(left):
+        if c:
+            g.wait_ge(S["k%d" % x], c)
     g.wait_ge(S.ls, n)
 
-    got = count(off) + count(rest)
+    got = count(topo.mask(twin, core) if topo.mask(twin, core) else off) + count(MM["rest"])
+    w = LC // 4
     v.wait_ge(S.ssel, 1)
-    v.wait_ge(S.sfa, got)
-    v.tensor_copy(T.yb[:, 0:HALF], T.fa[:].indirect(T.sel[:, 0:h])).then_inc(S.sya, 1)
     s.wait_ge(S.ssel, 1)
-    s.wait_ge(S.sfb, got)
-    s.activation(T.yb[:, HALF:ENT], T.fb[:].indirect(T.sel[:, h:LC]), ActivationFunctionType.Copy).then_inc(S.syb, 1)
-    s.wait_ge(S.syb, 1)
-    s.dma_start(T.y[:, HALF:ENT], T.yb[:, HALF:ENT]).then_inc(S.sst, 16)
-    g.sync.wait_ge(S.sya, 1)
-    g.sync.dma_start(T.y[:, 0:HALF], T.yb[:, 0:HALF]).then_inc(S.sst, 16)
+    for k in range(4):
+        e, f, sy = (v, s)[k % 2], T["f%d" % k], S["sy%d" % k]
+        e.wait_ge(S["sf%d" % k], got)
+        o, i = T.yb[:, Q * k:Q * k + Q], f[:].indirect(T.sel[:, w * k:w * k + w])
+        if k % 2 == 0:
+            v.tensor_copy(o, i).then_inc(sy, 1)
+        else:
+            s.activation(o, i, ActivationFunctionType.Copy).then_inc(sy, 1)
+    for k in range(2):
+        e = (g.sync, s)[k]
+        e.wait_ge(S["sy%d" % (2 * k)], 1)
+        e.wait_ge(S["sy%d" % (2 * k + 1)], 1)
+        e.dma_start(T.y[:, HALF * k:HALF * k + HALF], T.yb[:, HALF * k:HALF * k + HALF]).then_inc(S.sst, 16)
     g.sync.wait_ge(S.sst, 32)
 
 
 def helper_core(g, core, T, topo, rank):
     S, nb = T.sem, neighbours(T, topo, rank)
     rc, rack, cable, twin = T.cores[rank], nb["rack"], nb["cable"], nb["twin"]
-    quarter, merge = helpers(T, topo, rc, twin)
-    if core not in quarter:
-        return
-    k = quarter.index(core)
-    xr = helpers(T, topo, rack, neighbours(T, topo, T.cores.index(rack))["twin"])[1][k // 2]
-    xc = helpers(T, topo, cable, neighbours(T, topo, T.cores.index(cable))["twin"])[1][k // 2]
-    lo = Q * (k % 2)
-    n = 0
-    off0 = topo.mask(rc, rack) & topo.mask(rc, cable)
-    onc0 = topo.mask(rc, merge[0])
-    rest0 = onc0 & ~off0
-    g.wait_ge(S.syr, count(onc0) // 4)
-    moff = topo.mask(core, xr)
-    n += send(g, topo, core, S.ls, [(xr, [T.yr[:]], T.xs[:, lo:lo + Q], S.sxs, moff)])
-    g.wait_ge(S.syc, count(rest0) // 4)
-    g.wait_ge(S.syd, count(off0) // 4)
-    n += send(g, topo, core, S.ls, [(xc, [T.yc[:], T.yd[:]], T.xc[:, lo:lo + Q], S.sxc, topo.mask(core, xc))])
+    quarter, merge, passer = roles(T, topo, rc)
+    rmerge = roles(T, topo, rack)[1]
+    MM = masks(topo, rc, rack, cable, core)
+    moff = topo.mask(core, rack)
+    hs = everyone(T, topo, rc)
+    w = hs.index(core)
+    np = 8 - w if core == hs[-1] else 1
+    g.wait_ge(S.sdq, np * count(MM["rest"]) // 8)
+    m = split(moff, np)
+    n = send(g, topo, core, S.ls, [(rack, [T.dq[j]], T.dr[w + j], S.sdr, m[j]) for j in range(np)])
+    if core in quarter:
+        k = quarter.index(core)
+        xc = roles(T, topo, cable)[1][k]
+        g.wait_ge(S.syc, engines(MM, "c", k))
+        g.wait_ge(S.syd, engines(MM, "d", k))
+        n += send(g, topo, core, S.ls, [(xc, [T.yc[:], T.yd[:]], T.xc[:], S.sxc, topo.mask(core, xc))])
+    if core == passer:
+        g.wait_ge(S.syr, count(MM["rest"]))
+        m = split(moff, 2)
+        n += send(g, topo, core, S.ls, [(rmerge[2 + j], [T.yr[:, Q * j:Q * j + Q]], T.xs[:], S.sxs, m[j]) for j in range(2)])
     if core in merge:
-        half = merge.index(core)
-        land, sem = ((T.fa, S.sfa), (T.fb, S.sfb))[half]
+        k = merge.index(core)
+        land, sem = T["f%d" % k], S["sf%d" % k]
         v = g.vector
-        v.wait_ge(S.sxo, count(rest0) // 2)
-        v.wait_ge(S.sxs, 2 * count(moff))
+        v.wait_ge(S.sxo, engines(MM, "o", k))
+        v.wait_ge(S.sxs, engines(MM, "x", k) if k < 2 else count(moff) // 2)
         v.tensor_tensor(T.xp[:], T.xo[:], T.xs[:], AluOpType.add).then_inc(S.sxp, 1)
         g.wait_ge(S.sxp, 1)
-        g.wait_ge(S.sxc, 2 * count(topo.mask(core, xc)))
+        g.wait_ge(S.sxc, count(topo.mask(core, cable)))
         mt = topo.mask(core, twin)
-        n += send(g, topo, core, S.ls, [(twin, [T.xp[:], T.xc[:]], land[:, HALF:2 * HALF], sem, mt)])
-        n += send(g, topo, core, S.ls, [(rc, [T.xp[:], T.xc[:]], land[:, 0:HALF], sem, topo.mask(core, rc) & ~mt)])
+        n += send(g, topo, core, S.ls, [(twin, [T.xp[:], T.xc[:]], land[:, Q:2 * Q], sem, mt)])
+        n += send(g, topo, core, S.ls, [(rc, [T.xp[:], T.xc[:]], land[:, 0:Q], sem, topo.mask(core, rc) & ~mt)])
     g.wait_ge(S.ls, n)
 
 

from concourse.bass import DstId, RemoteDMATransfer
from concourse.mybir import dt, AluOpType, ActivationFunctionType

ROWS, COLS, ENT = 128, 4096, 1024
Q, HALF = 256, 512
LC = 64
SCHED = [("c", (0, 1), "rest", ()), ("c", (2, 3), "rest", ()), ("d", (0, 1), "off", ()), ("d", (2, 3), "off", ()),
         ("r", (2,), "rest", ()), ("x", (0, 1), "off", (2,)), ("o", (0, 1), "rest", (1,)), ("o", (2, 3), "all", (4,))]

SCRATCH = {
    "tabw": ("sbuf", [128, COLS + 8], "float32"),
    "lo": ("sbuf", [128, LC], "int32"), "lr": ("sbuf", [128, LC], "int32"),
    "lc": ("sbuf", [128, LC], "int32"), "ld": ("sbuf", [128, LC], "int32"),
    "to": ("sbuf", [128, LC], "int32"), "tr": ("sbuf", [128, LC], "int32"),
    "tc": ("sbuf", [128, LC], "int32"), "td": ("sbuf", [128, LC], "int32"),
    "oo": ("sbuf", [128, LC], "uint16"), "orr": ("sbuf", [128, LC], "uint16"),
    "oc": ("sbuf", [128, LC], "uint16"), "od": ("sbuf", [128, LC], "uint16"),
    "go": ("sbuf", [128, ENT], "float32"), "gr": ("sbuf", [128, ENT], "float32"),
    "gc4": ("sbuf", [128, ENT], "float32"), "gd": ("sbuf", [128, ENT], "float32"),
    "jp": ("sbuf", [128, LC], "int32"), "jc": ("sbuf", [128, LC], "int32"), "jq": ("sbuf", [128, LC], "int32"),
    "jj": ("sbuf", [128, LC], "int32"), "sd": ("sbuf", [128, LC], "int32"), "sm": ("sbuf", [128, LC], "int32"),
    "ss": ("sbuf", [128, LC], "int32"), "sel": ("sbuf", [128, LC], "uint16"),
    "f0": ("sbuf", [128, 2 * Q], "float32"), "f1": ("sbuf", [128, 2 * Q], "float32"),
    "f2": ("sbuf", [128, 2 * Q], "float32"), "f3": ("sbuf", [128, 2 * Q], "float32"),
    "yb": ("sbuf", [128, ENT], "float32"),
    "dl": ("dram", [8, 128, 1], "int32"), "dr": ("dram", [8, 128, 1], "int32"),
    "dq": ("dram", [2, 128, 1], "int32"),
    "yc": ("sbuf", [128, Q], "float32"), "yd": ("sbuf", [128, Q], "float32"),
    "yr": ("sbuf", [128, HALF], "float32"),
    "xo": ("sbuf", [128, Q], "float32"), "xs": ("sbuf", [128, Q], "float32"),
    "xc": ("sbuf", [128, Q], "float32"), "xp": ("sbuf", [128, Q], "float32"),
}
SEMAPHORES = ["sidx", "stab", "sio", "vf", "vq", "slr", "slc", "sld", "ls", "sdl", "sdr", "sdq",
              "k0", "k1", "k2", "k3", "k4", "k5", "k6", "k7", "k8", "k9",
              "foo", "for_", "foc", "fod", "ho", "hr", "hc", "hd", "ssel",
              "syr", "syc", "syd", "sxo", "sxs", "sxc", "sxp", "sf0", "sf1", "sf2", "sf3",
              "sy0", "sy1", "sy2", "sy3", "sst"]


def place(topo, c):
    return (topo.host(c), topo.chip(c))


def neighbours(T, topo, r):
    me, out = T.cores[r], {}
    for c in T.cores:
        if c == me:
            continue
        if topo.host(c) == topo.host(me):
            out["twin"] = c
        elif topo.chip(c) == topo.chip(me):
            if topo.rack(topo.host(c)) == topo.rack(topo.host(me)):
                out["rack"] = c
            elif topo.may_write(me, c):
                out["cable"] = c
    return out


def roles(T, topo, rc):
    twin = neighbours(T, topo, T.cores.index(rc))["twin"]
    per = 512 // 4
    base = topo.host(rc) * per
    chip = [c for c in range(base, base + per) if topo.chip(c) == topo.chip(rc) and c != rc]
    quarter, merge, other = [], [], []
    for d in (topo.die(rc), 1 - topo.die(rc)):
        own = [c for c in chip if topo.die(c) == d and topo.may_write(c, twin)]
        non = [c for c in chip if topo.die(c) == d and not topo.may_write(c, twin)]
        quarter += [non[0], own[0]]
        merge += own
        other += non[1:]
    return quarter, merge, other[0]


def everyone(T, topo, rc):
    q, m, p = roles(T, topo, rc)
    return q + [c for c in m if c not in q] + [p]


def split(mask, n):
    bits = [b for b in range(16) if mask >> b & 1]
    k = len(bits) // n
    return [sum(1 << b for b in bits[i * k:(i + 1) * k]) for i in range(n)]


def count(mask):
    return sum(mask >> b & 1 for b in range(16))


def masks(topo, rc, rack, cable, helper):
    off = topo.mask(rc, rack) & topo.mask(rc, cable)
    onc = topo.mask(rc, helper)
    return {"all": onc, "off": off, "rest": onc & ~off}


def engines(MM, block, k):
    return [count(MM[mk]) // len(qq) for b, qq, mk, hold in SCHED if b == block and k in qq][0]


def send(g, topo, core, local, parts):
    trs, n = [], 0
    for dst, srcs, out, sem, mask in parts:
        rid, pid = topo.addr(dst, core)
        trs.append(RemoteDMATransfer(dst_ids=[DstId(rid=rid, pnc=pid)], dma_engine_mask=mask, remote_sem=sem,
                                     srcs=srcs, dsts=[out], alu_op=1 if len(srcs) > 1 else 0))
        n += count(mask)
    g.remote_dma_fused(trs, local_sem=local)
    return n


def rank_core(g, core, T, topo, rank):
    S, nb = T.sem, neighbours(T, topo, rank)
    rack, cable, twin = nb["rack"], nb["cable"], nb["twin"]
    quarter, merge, passer = roles(T, topo, core)
    rquarter, rmerge, _ = roles(T, topo, rack)
    v, s = g.vector, g.scalar
    add, mult, mx, mn = AluOpType.add, AluOpType.mult, AluOpType.max, AluOpType.min

    for k in range(8):
        (g.sync if k % 2 == 0 else s).dma_start(T.lo[16 * k:16 * k + 16, :], T.idx[:]).then_inc(S.sidx, 16)
    g.sync.dma_start(T.dl[:], T.idx[:]).then_inc(S.sdl, 16)
    g.sync.dma_start(T.tabw[0:64, 4:4 + COLS], T.tab[0:64, :]).then_inc(S.stab, 16)
    s.dma_start(T.tabw[64:128, 4:4 + COLS], T.tab[64:128, :]).then_inc(S.stab, 16)
    hs = everyone(T, topo, core)
    g.sync.wait_ge(S.sdr, len(hs) * count(topo.mask(rack, core)))
    for k in range(8):
        g.sync.dma_start(T.lr[16 * k:16 * k + 16, :], T.dr[:]).then_inc(S.slr, 16)

    g.iota(T.jp[:], [[0, LC]], 0, 1).then_inc(S.sio, 1)
    g.iota(T.jc[:], [[0, 2], [0, 2], [16, LC // 4]], 0, 0).then_inc(S.sio, 1)
    MM = masks(topo, core, rack, cable, merge[0])
    off = MM["off"]
    n = 0
    g.wait_ge(S.sidx, 128)
    n += send(g, topo, core, S.ls, [(cable, [T.lo[:]], T.lc[:], S.slc, off)])
    g.wait_ge(S.sdl, 16)
    m = split(MM["rest"], 8)
    last = len(hs) - 1
    n += send(g, topo, core, S.ls, [(hs[min(k, last)], [T.dl[k]], T.dq[k - min(k, last)], S.sdq, m[k]) for k in range(8)])
    g.wait_ge(S.slc, count(off))
    n += send(g, topo, core, S.ls, [(rack, [T.lc[:]], T.ld[:], S.sld, off)])

    nq = [0]

    def chain(ins):
        ins.then_inc(S.vq, 1)
        nq[0] += 1
        v.wait_ge(S.vq, nq[0])

    v.memset(T.tabw[:, 0:4], -0.0).then_inc(S.vf, 1)
    v.memset(T.tabw[:, 4 + COLS:8 + COLS], -0.0).then_inc(S.vf, 1)

    def offsets(lst, tmp, out, sem):
        chain(v.tensor_scalar(tmp[:], lst[:], float(1 - COLS * rank), 0.0, add, mx))
        v.tensor_scalar(out[:], tmp[:], float(COLS + 1), None, mn).then_inc(sem, 1)

    v.wait_ge(S.sidx, 128)
    offsets(T.lo, T.to, T.oo, S.foo)
    v.wait_ge(S.sio, 2)
    chain(v.tensor_scalar(T.jq[:], T.jp[:], 15, None, AluOpType.bitwise_and))
    chain(v.tensor_tensor(T.jj[:], T.jq[:], T.jc[:], add))
    chain(v.tensor_scalar(T.sd[:], T.lo[:], 12, 1, AluOpType.logical_shift_right, AluOpType.bitwise_and))
    mine = rank % 2
    chain(v.tensor_scalar(T.sm[:], T.sd[:], float(Q if mine == 0 else -Q), float(0 if mine == 0 else Q), mult, add))
    chain(v.tensor_tensor(T.ss[:], T.jj[:], T.sm[:], add))
    v.tensor_copy(T.sel[:], T.ss[:]).then_inc(S.ssel, 1)
    win = T.tabw[:, 3:5 + COLS]
    h = LC // 2
    done = {"c": S.hc, "d": S.hd, "r": S.hr, "x": S.hr, "o": S.ho}

    def gather(b, o, out, ready):
        v.wait_ge(ready, 1)
        v.tensor_copy(out[:, 0:HALF], win.indirect(o[:, 0:h])).then_inc(done[b], 1)
        s.wait_ge(ready, 1)
        s.activation(out[:, HALF:ENT], win.indirect(o[:, h:LC]), ActivationFunctionType.Copy).then_inc(done[b], 1)

    v.wait_ge(S.slc, count(off))
    offsets(T.lc, T.tc, T.oc, S.foc)
    for e in (v, s):
        e.wait_ge(S.vf, 2)
        e.wait_ge(S.stab, 32)
    gather("c", T.oc, T.gc4, S.foc)
    v.wait_ge(S.sld, count(off))
    offsets(T.ld, T.td, T.od, S.fod)
    gather("d", T.od, T.gd, S.fod)
    v.wait_ge(S.slr, 128)
    offsets(T.lr, T.tr, T.orr, S.for_)
    gather("r", T.orr, T.gr, S.for_)
    gather("o", T.oo, T.go, S.foo)

    to = {"c": (quarter, T.gc4, T.yc, S.syc), "d": (rquarter, T.gd, T.yd, S.syd), "x": (rmerge, T.gr, T.xs, S.sxs),
          "o": (merge, T.go, T.xo, S.sxo)}
    left = []
    for i, (b, qq, mk, hold) in enumerate(SCHED):
        g.wait_ge(done[b], 2)
        for x in hold:
            g.wait_ge(S["k%d" % x], left[x])
            left[x] = 0
        m = split(MM[mk], len(qq))
        if b == "r":
            parts = [(passer, [T.gr[:, Q * qq[0]:Q * qq[0] + HALF]], T.yr[:], S.syr, m[0])]
        else:
            cs, src, land, sem = to[b]
            parts = [(cs[k], [src[:, Q * k:Q * k + Q]], land[:], sem, m[a]) for a, k in enumerate(qq)]
        left.append(send(g, topo, core, S["k%d" % i], parts))
    for x, c in enumerate(left):
        if c:
            g.wait_ge(S["k%d" % x], c)
    g.wait_ge(S.ls, n)

    got = count(topo.mask(twin, core) if topo.mask(twin, core) else off) + count(MM["rest"])
    w = LC // 4
    v.wait_ge(S.ssel, 1)
    s.wait_ge(S.ssel, 1)
    for k in range(4):
        e, f, sy = (v, s)[k % 2], T["f%d" % k], S["sy%d" % k]
        e.wait_ge(S["sf%d" % k], got)
        o, i = T.yb[:, Q * k:Q * k + Q], f[:].indirect(T.sel[:, w * k:w * k + w])
        if k % 2 == 0:
            v.tensor_copy(o, i).then_inc(sy, 1)
        else:
            s.activation(o, i, ActivationFunctionType.Copy).then_inc(sy, 1)
    for k in range(2):
        e = (g.sync, s)[k]
        e.wait_ge(S["sy%d" % (2 * k)], 1)
        e.wait_ge(S["sy%d" % (2 * k + 1)], 1)
        e.dma_start(T.y[:, HALF * k:HALF * k + HALF], T.yb[:, HALF * k:HALF * k + HALF]).then_inc(S.sst, 16)
    g.sync.wait_ge(S.sst, 32)


def helper_core(g, core, T, topo, rank):
    S, nb = T.sem, neighbours(T, topo, rank)
    rc, rack, cable, twin = T.cores[rank], nb["rack"], nb["cable"], nb["twin"]
    quarter, merge, passer = roles(T, topo, rc)
    rmerge = roles(T, topo, rack)[1]
    MM = masks(topo, rc, rack, cable, core)
    moff = topo.mask(core, rack)
    hs = everyone(T, topo, rc)
    w = hs.index(core)
    np = 8 - w if core == hs[-1] else 1
    g.wait_ge(S.sdq, np * count(MM["rest"]) // 8)
    m = split(moff, np)
    n = send(g, topo, core, S.ls, [(rack, [T.dq[j]], T.dr[w + j], S.sdr, m[j]) for j in range(np)])
    if core in quarter:
        k = quarter.index(core)
        xc = roles(T, topo, cable)[1][k]
        g.wait_ge(S.syc, engines(MM, "c", k))
        g.wait_ge(S.syd, engines(MM, "d", k))
        n += send(g, topo, core, S.ls, [(xc, [T.yc[:], T.yd[:]], T.xc[:], S.sxc, topo.mask(core, xc))])
    if core == passer:
        g.wait_ge(S.syr, count(MM["rest"]))
        m = split(moff, 2)
        n += send(g, topo, core, S.ls, [(rmerge[2 + j], [T.yr[:, Q * j:Q * j + Q]], T.xs[:], S.sxs, m[j]) for j in range(2)])
    if core in merge:
        k = merge.index(core)
        land, sem = T["f%d" % k], S["sf%d" % k]
        v = g.vector
        v.wait_ge(S.sxo, engines(MM, "o", k))
        v.wait_ge(S.sxs, engines(MM, "x", k) if k < 2 else count(moff) // 2)
        v.tensor_tensor(T.xp[:], T.xo[:], T.xs[:], AluOpType.add).then_inc(S.sxp, 1)
        g.wait_ge(S.sxp, 1)
        g.wait_ge(S.sxc, count(topo.mask(core, cable)))
        mt = topo.mask(core, twin)
        n += send(g, topo, core, S.ls, [(twin, [T.xp[:], T.xc[:]], land[:, Q:2 * Q], sem, mt)])
        n += send(g, topo, core, S.ls, [(rc, [T.xp[:], T.xc[:]], land[:, 0:Q], sem, topo.mask(core, rc) & ~mt)])
    g.wait_ge(S.ls, n)


def rank_program(g, core, T, topo):
    rank = T.rank_of(core)
    if rank is not None:
        rank_core(g, core, T, topo, rank)
        return
    for r in range(len(T.cores)):
        if place(topo, T.cores[r]) == place(topo, core):
            helper_core(g, core, T, topo, r)
